import numpy as np, ml_dtypes
CORES = [2,3,42,43,82,83,122,123]
N = 8
import mx_ref
BF = ml_dtypes.bfloat16
def gentries(a):
    return np.ascontiguousarray(a.reshape(8, 16, -1).transpose(0, 2, 1)).reshape(8, -1)
def gtable(e):
    e = np.asarray(e); return np.ascontiguousarray(e.reshape(8, -1, 16).transpose(0, 2, 1)).reshape(128, -1).astype(np.int32)
def gcols(t, e):
    v = np.concatenate([t.reshape(8, 16, -1, 4), np.zeros((8, 16, 1, 4), BF)], axis=2)
    return np.ascontiguousarray(np.stack([v[g][:, e[g]] for g in range(8)])).reshape(128, -1)
def f(rng, *shape):
    return mx_ref.flush((rng.standard_normal(shape, dtype=np.float32) * np.exp2(rng.integers(-2, 3, shape[:-1] + (1,)))).astype(BF))
def wide(rng, *shape, cols=0):
    v = rng.standard_normal(shape, dtype=np.float32) * np.exp2(rng.integers(-12, 13, shape)).astype(np.float32)
    if cols: v *= np.repeat(np.exp2(rng.integers(-cols, cols + 1, shape[:-2] + (1, shape[-1] // 4))) * (rng.random(shape[:-2] + (1, shape[-1] // 4)) > 0.0625), 4, axis=-1).astype(np.float32)
    return mx_ref.flush(v.astype(BF))
S = 256
def block(rng, how):
    if how == "one": return np.full((8, S), rng.integers(0, 128))
    if how == "groups": return np.tile(rng.integers(0, 128, S), (8, 1))
    if how == "ends": return np.stack([rng.permutation(np.arange(S) % 2 * 127) for g in range(8)])
    if how == "distinct": return np.stack([np.tile(rng.permutation(128), S // 128) for g in range(8)])
    return rng.integers(0, 128, (8, S))
def lists(rng, how=""):
    return {"cw": np.stack([gtable(np.concatenate([block(rng, how) for s in range(N)], axis=1)) for r in range(N)])}
def setup_inputs(rng):
    return {"bk": f(rng, N, 128, 512), "x": f(rng, N, 128, 512 * N), **lists(rng)}
def setup_inputs_one(rng):
    return {**setup_inputs(rng), **lists(rng, "one")}
def setup_inputs_groups(rng):
    return {**setup_inputs(rng), **lists(rng, "groups")}
def setup_inputs_ends(rng):
    return {**setup_inputs(rng), **lists(rng, "ends")}
def setup_inputs_distinct(rng):
    return {**setup_inputs(rng), **lists(rng, "distinct")}
def setup_inputs_spread(rng):
    d = setup_inputs(rng); d["bk"] = wide(rng, N, 128, 512, cols=4); d["x"] = wide(rng, N, 128, 512 * N); return d
def check_inputs(d):
    b = []
    for r in range(N):
        e = d["cw"][r]
        if e.min() < 0 or e.max() > 127: b.append("cw")
    return b
def reference(bk, x, cw):
    y = np.zeros((N, 128, S), np.float32)
    for r in range(N):
        e = gentries(cw[r])
        for s in range(N):
            W = gcols(bk[s], e[:, S * s:S * s + S])
            X = np.ascontiguousarray(x[r][:, 512 * s:512 * s + 512])
            y[r] += mx_ref.matmul(mx_ref.quantize(X), mx_ref.quantize(W))
    return {"y": y}

@@ -1,0 +1,227 @@
+from concourse.mybir import dt, AluOpType, ActivationFunctionType
+from concourse.bass import DstId, RemoteDMATransfer
+
+N = 8
+S = 256
+L = S // 16
+ORDER = (2, 3, 6, 7, 4, 5, 1)
+STEPS = ((0, 1), (2, 3), (4, 5), (6,))
+ARRIVAL = (0, 2, 1, 4, 3, 6, 5)
+
+SCRATCH = {
+    "cwi": ("sbuf", [128, N * L], "int32"),
+    "cwu": ("sbuf", [128, N * L], "uint16"),
+    "lst": ("sbuf", [128, 7 * L], "uint16"),
+    "bks": ("sbuf", [128, 512], "bfloat16"),
+    "bkp": ("sbuf", [128, 512], "bfloat16"),
+    "xs": ("sbuf", [128, 512 * N], "bfloat16"),
+    "xq": ("sbuf", [128, 128 * N], "float8_e4m3fn_x4"),
+    "xz": ("sbuf", [128, 128 * N], "uint8"),
+    "w": ("sbuf", [128, 4 * S * N], "bfloat16"),
+    "wq": ("sbuf", [128, S * N], "float8_e4m3fn_x4"),
+    "wz": ("sbuf", [128, S * N], "uint8"),
+    "rq": ("sbuf", [128, S * 7], "float8_e4m3fn_x4"),
+    "rz": ("sbuf", [128, S * 7], "uint8"),
+    "yp": ("psum", [128, 512], "float32"),
+    "ys": ("sbuf", [128, S], "float32"),
+}
+SEMAPHORES = (["ldc", "ldb", "ldx0", "ldx1", "conv", "plv", "pls", "lsent", "wsent", "fsent", "qself", "gvs", "gss",
+               "xq0", "xq1", "mm", "cp", "st"]
+              + ["l%d" % k for k in range(7)] + ["a%d" % k for k in range(7)]
+              + ["rc%d" % k for k in range(14)] + ["rz%d" % k for k in range(14)]
+              + ["gv%d" % i for i in range(4)] + ["gs%d" % i for i in range(4)] + ["q%d" % i for i in range(4)])
+
+
+def bits(engines):
+    return sum(1 << e for e in engines)
+
+
+def relay_of(rank, slot, T, topo):
+    src, dst = T.cores[rank], T.cores[rank ^ ORDER[slot]]
+    if topo.chip(src) == topo.chip(dst) or slot % 2 == 0:
+        return None
+    far = [T.cores[rank ^ d] for d in ORDER]
+    cand = [c for c in topo.cores_of(src)
+            if topo.die(c) != topo.die(src) and T.rank_of(c) is None and all(topo.may_write(c, d) for d in far if d != c)]
+    mine = [c for c in T.cores if topo.chip(c) == topo.chip(src)]
+    return cand[mine.index(src) % len(cand)]
+
+
+def dest(core, topo):
+    rid, pid, _ = topo.addr(core)
+    return DstId(rid=rid, pnc=pid)
+
+
+def forward(g, core, T, topo):
+    total = 0
+    for slot in range(7):
+        for rank in range(N):
+            if relay_of(rank, slot, T, topo) != core:
+                continue
+            dst = T.cores[rank ^ ORDER[slot]]
+            rid, pid, _ = topo.addr(dst)
+            mask = topo.mask(core, dst)
+            n = len(topo.engines(core, dst))
+            came = relay_engines(T.cores[rank], core, dst, topo)
+            c = slice(slot * S, slot * S + S)
+            view = T.rq[:, c].bitcast(dt.uint8)
+            g.wait_ge(T.sem["rc%d" % slot], len(came))
+            g.remote_dma(out_ap=view, in_ap=view, remote_sem=T.sem["a%d" % slot], local_sem=T.sem.fsent,
+                         pid=pid, routing_id=rid, dma_engine_mask=mask)
+            g.wait_ge(T.sem["rz%d" % slot], len(came))
+            g.remote_dma(out_ap=T.rz[:, c], in_ap=T.rz[:, c], remote_sem=T.sem["a%d" % slot], local_sem=T.sem.fsent,
+                         pid=pid, routing_id=rid, dma_engine_mask=mask)
+            total += 2 * n
+    if total:
+        g.wait_ge(T.sem.fsent, total)
+
+
+def relay_engines(src, via, dst, topo):
+    off = topo.engines(src, dst)
+    return [e for e in topo.engines(src, via) if e not in off]
+
+
+def rank_program(g, core, T, topo):
+    rank = T.rank_of(core)
+    if rank is None:
+        forward(g, core, T, topo)
+        return
+    sem = T.sem
+    far0 = T.cores[rank ^ ORDER[0]]
+    off = topo.engines(core, far0)
+    half = len(off) // 2
+    COPY = ActivationFunctionType.Copy
+
+    g.sync.dma_start(T.cwi[:], T.cw[:]).then_inc(sem.ldc, 16)
+    h = 512 * N // 2
+    g.sync.dma_start(T.xs[:, 0:h], T.x[:, 0:h]).then_inc(sem.ldx0, 16)
+
+    g.wait_ge(sem.conv, 1)
+    lsent = 0
+    mate = T.cores[rank ^ ORDER[6]]
+    rest = relay_engines(core, mate, far0, topo)
+    for i in range(3):
+        part = [(STEPS[i][0], off[:half]), (STEPS[i][1], off[half:])]
+        if i == 2:
+            part.append((6, rest))
+        tr = []
+        for slot, eng in part:
+            p = rank ^ ORDER[slot]
+            tr.append(RemoteDMATransfer(dst_ids=[dest(T.cores[p], topo)], dma_engine_mask=bits(eng),
+                                        remote_sem=sem["l%d" % slot], src=T.cwu[:, p * L:p * L + L],
+                                        dst=T.lst[:, slot * L:slot * L + L]))
+            lsent += len(eng)
+        g.remote_dma_fused(tr, local_sem=sem.lsent)
+    g.sync.wait_ge(sem.lsent, lsent)
+    g.sync.dma_start(T.xs[:, h:2 * h], T.x[:, h:2 * h]).then_inc(sem.ldx1, 16)
+
+    wsent = 0
+    for i, step in enumerate(STEPS):
+        g.wait_ge(sem["q%d" % i], 1)
+        for what in range(2):
+            tr = []
+            for slot in step:
+                dst = T.cores[rank ^ ORDER[slot]]
+                via = relay_of(rank, slot, T, topo)
+                a = (slot + 1) * S
+                if what == 0:
+                    src, out = T.wq[:, a:a + S].bitcast(dt.uint8), T.rq[:, slot * S:slot * S + S].bitcast(dt.uint8)
+                else:
+                    src, out = T.wz[:, a:a + S], T.rz[:, slot * S:slot * S + S]
+                if via is None:
+                    to, s = dst, sem["a%d" % slot]
+                    eng = rest if slot == 6 else off
+                else:
+                    to, s = via, sem[("rc%d" if what == 0 else "rz%d") % slot]
+                    eng = relay_engines(core, via, dst, topo)
+                tr.append(RemoteDMATransfer(dst_ids=[dest(to, topo)], dma_engine_mask=bits(eng), remote_sem=s,
+                                            src=src, dst=out))
+                wsent += len(eng)
+            g.remote_dma_fused(tr, local_sem=sem.wsent)
+    g.wait_ge(sem.wsent, wsent)
+
+    g.scalar.dma_start(T.bks[:], T.bk[:]).then_inc(sem.ldb, 16)
+    g.scalar.wait_ge(sem.ldb, 16)
+    for t in (2, 3):
+        g.scalar.activation(T.bkp[:, t * 128:t * 128 + 128], T.bks[:, t:512:4], COPY).then_inc(sem.pls, 1)
+
+    def window(t):
+        return T.bkp[:, t * 128:t * 128 + 128]
+
+    def place(t, slot, n):
+        a = (slot + 1) * 4 * S
+        return T.w[:, a + t:a + n * 4 * S:4]
+
+    mylist = T.cwu[:, rank * L:rank * L + L]
+    g.scalar.wait_ge(sem.pls, 2)
+    g.scalar.wait_ge(sem.conv, 1)
+    for t in (2, 3):
+        g.scalar.activation(place(t, -1, 1), window(t).indirect(mylist), COPY).then_inc(sem.gss, 1)
+    g.scalar.wait_ge(sem.plv, 2)
+    for i, step in enumerate(STEPS):
+        n, a = len(step), step[0]
+        for slot in step:
+            g.scalar.wait_ge(sem["l%d" % slot], half if slot < 6 else len(rest))
+        lists = T.lst[:, a * L:(a + n) * L]
+        for t in (2, 3):
+            g.scalar.activation(place(t, a, n), window(t).indirect(lists), COPY).then_inc(sem["gs%d" % i], 1)
+        if n == 2:
+            b = step[1]
+            g.scalar.activation(place(1, b, 1), window(1).indirect(T.lst[:, b * L:b * L + L]), COPY).then_inc(sem["gs%d" % i], 1)
+
+    g.vector.wait_ge(sem.ldc, 16)
+    g.vector.tensor_copy(T.cwu[:], T.cwi[:]).then_inc(sem.conv, 1)
+    g.vector.wait_ge(sem.ldb, 16)
+    for t in (0, 1):
+        g.vector.tensor_copy(T.bkp[:, t * 128:t * 128 + 128], T.bks[:, t:512:4]).then_inc(sem.plv, 1)
+    g.vector.wait_ge(sem.plv, 2)
+    g.vector.wait_ge(sem.conv, 1)
+    for t in (0, 1):
+        g.vector.tensor_copy(place(t, -1, 1), window(t).indirect(mylist)).then_inc(sem.gvs, 1)
+    g.vector.wait_ge(sem.gvs, 2)
+    g.vector.wait_ge(sem.gss, 2)
+    g.vector.quantize_mx(T.wq[:, 0:S], T.wz[:, 0:S], T.w[:, 0:4 * S]).then_inc(sem.qself, 1)
+
+    def quantise_x(b):
+        g.vector.wait_ge(sem["ldx%d" % b], 16)
+        c = slice(b * 512, b * 512 + 512)
+        g.vector.quantize_mx(T.xq[:, c], T.xz[:, c], T.xs[:, b * 2048:b * 2048 + 2048]).then_inc(sem["xq%d" % b], 1)
+
+    quantise_x(0)
+    for i, step in enumerate(STEPS):
+        n, a = len(step), step[0]
+        if i == 3:
+            quantise_x(1)
+        for slot in step:
+            g.vector.wait_ge(sem["l%d" % slot], half if slot < 6 else len(rest))
+        g.vector.tensor_copy(place(0, a, n), window(0).indirect(T.lst[:, a * L:(a + n) * L])).then_inc(sem["gv%d" % i], 1)
+        g.vector.tensor_copy(place(1, a, 1), window(1).indirect(T.lst[:, a * L:a * L + L])).then_inc(sem["gv%d" % i], 1)
+        g.vector.wait_ge(sem["gv%d" % i], 2)
+        g.vector.wait_ge(sem["gs%d" % i], 2 if n == 1 else 3)
+        c = slice((a + 1) * S, (a + 1 + n) * S)
+        g.vector.quantize_mx(T.wq[:, c], T.wz[:, c],
+                             T.w[:, (a + 1) * 4 * S:(a + 1 + n) * 4 * S]).then_inc(sem["q%d" % i], 1)
+
+    def product(s, codes, scales, start, stop):
+        c = slice(s * 128, s * 128 + 128)
+        r = g.tensor.matmul_mx(T.yp[:, 0:S], T.xq[:, c], T.xz[:, c], codes, scales, start, stop)
+        if stop:
+            r.then_inc(sem.mm, 1)
+
+    g.tensor.wait_ge(sem.xq0, 1)
+    g.tensor.wait_ge(sem.xq1, 1)
+    g.tensor.wait_ge(sem.qself, 1)
+    product(rank, T.wq[:, 0:S], T.wz[:, 0:S], True, False)
+    for j, slot in enumerate(ARRIVAL):
+        via = relay_of(rank ^ ORDER[slot], slot, T, topo)
+        src = T.cores[rank ^ ORDER[slot]]
+        count = len(rest) if slot == 6 else len(topo.engines(src if via is None else via, core))
+        g.tensor.wait_ge(sem["a%d" % slot], 2 * count)
+        c = slice(slot * S, slot * S + S)
+        product(rank ^ ORDER[slot], T.rq[:, c], T.rz[:, c], False, j == 6)
+
+    g.vector.wait_ge(sem.mm, 1)
+    g.vector.tensor_copy(T.ys[:], T.yp[:, 0:S]).then_inc(sem.cp, 1)
+    g.sync.wait_ge(sem.cp, 1)
+    g.sync.dma_start(T.y[:], T.ys[:]).then_inc(sem.st, 16)
+    g.sync.wait_ge(sem.st, 16)

@@ -4,9 +4,12 @@ from concourse.bass import DstId, RemoteDMATransfer
 N = 8
 S = 256
 L = S // 16
-ORDER = (2, 3, 6, 7, 4, 5, 1)
-STEPS = ((0, 1), (2, 3), (4, 5), (6,))
-ARRIVAL = (0, 2, 1, 4, 3, 6, 5)
+ORDER = (3, 2, 5, 7, 6, 4, 1)
+VIA = (True, False, True, True, False, False, False)
+STEPS = ((0,), (1, 2), (3,), (4,), (5,), (6,))
+SHARE = ((2, 3), (2, 3, 1), (1, 2, 3), (2, 3), (1, 2, 3), (2, 3))
+LISTS = ((0, 1), (2, 3), (4, 5, 6))
+ARRIVAL = (1, 0, 2, 4, 3, 6, 5)
 
 SCRATCH = {
     "cwi": ("sbuf", [128, N * L], "int32"),
@@ -28,28 +31,44 @@ SCRATCH = {
 SEMAPHORES = (["ldc", "ldb", "ldx0", "ldx1", "conv", "plv", "pls", "lsent", "wsent", "fsent", "qself", "gvs", "gss",
                "xq0", "xq1", "mm", "cp", "st"]
               + ["l%d" % k for k in range(7)] + ["a%d" % k for k in range(7)]
-              + ["rc%d" % k for k in range(14)] + ["rz%d" % k for k in range(14)]
-              + ["gv%d" % i for i in range(4)] + ["gs%d" % i for i in range(4)] + ["q%d" % i for i in range(4)])
+              + ["rc%d" % k for k in range(7)] + ["rz%d" % k for k in range(7)]
+              + ["gv%d" % i for i in range(6)] + ["gs%d" % i for i in range(6)] + ["q%d" % i for i in range(6)])
 
 
 def bits(engines):
     return sum(1 << e for e in engines)
 
 
+def dest(core, topo):
+    rid, pid, _ = topo.addr(core)
+    return DstId(rid=rid, pnc=pid)
+
+
 def relay_of(rank, slot, T, topo):
-    src, dst = T.cores[rank], T.cores[rank ^ ORDER[slot]]
-    if topo.chip(src) == topo.chip(dst) or slot % 2 == 0:
+    if not VIA[slot]:
         return None
-    far = [T.cores[rank ^ d] for d in ORDER]
+    src, dst = T.cores[rank], T.cores[rank ^ ORDER[slot]]
     cand = [c for c in topo.cores_of(src)
-            if topo.die(c) != topo.die(src) and T.rank_of(c) is None and all(topo.may_write(c, d) for d in far if d != c)]
+            if T.rank_of(c) is None and topo.may_write(c, dst) and topo.die(c) != topo.die(src)]
+    reach = {c: sum(topo.may_write(c, d) for d in T.cores) for c in cand}
+    cand = [c for c in cand if reach[c] == min(reach.values())]
     mine = [c for c in T.cores if topo.chip(c) == topo.chip(src)]
     return cand[mine.index(src) % len(cand)]
 
 
-def dest(core, topo):
-    rid, pid, _ = topo.addr(core)
-    return DstId(rid=rid, pnc=pid)
+def off_chip(rank, T, topo):
+    return topo.engines(T.cores[rank], T.cores[rank ^ ORDER[0]])
+
+
+def first_engines(rank, slot, T, topo):
+    src, dst = T.cores[rank], T.cores[rank ^ ORDER[slot]]
+    off = off_chip(rank, T, topo)
+    via = relay_of(rank, slot, T, topo)
+    to = dst if via is None else via
+    if topo.chip(src) != topo.chip(to):
+        return off
+    engines = topo.engines(src, to)
+    return engines if slot == 0 else [e for e in engines if e not in off]
 
 
 def forward(g, core, T, topo):
@@ -61,24 +80,18 @@ def forward(g, core, T, topo):
             dst = T.cores[rank ^ ORDER[slot]]
             rid, pid, _ = topo.addr(dst)
             mask = topo.mask(core, dst)
-            n = len(topo.engines(core, dst))
-            came = relay_engines(T.cores[rank], core, dst, topo)
+            came = len(first_engines(rank, slot, T, topo))
             c = slice(slot * S, slot * S + S)
             view = T.rq[:, c].bitcast(dt.uint8)
-            g.wait_ge(T.sem["rc%d" % slot], len(came))
+            g.wait_ge(T.sem["rc%d" % slot], came)
             g.remote_dma(out_ap=view, in_ap=view, remote_sem=T.sem["a%d" % slot], local_sem=T.sem.fsent,
                          pid=pid, routing_id=rid, dma_engine_mask=mask)
-            g.wait_ge(T.sem["rz%d" % slot], len(came))
+            g.wait_ge(T.sem["rz%d" % slot], came)
             g.remote_dma(out_ap=T.rz[:, c], in_ap=T.rz[:, c], remote_sem=T.sem["a%d" % slot], local_sem=T.sem.fsent,
                          pid=pid, routing_id=rid, dma_engine_mask=mask)
-            total += 2 * n
+            total += 2 * len(topo.engines(core, dst))
     if total:
         g.wait_ge(T.sem.fsent, total)
-
-
-def relay_engines(src, via, dst, topo):
-    off = topo.engines(src, dst)
-    return [e for e in topo.engines(src, via) if e not in off]
 
 
 def rank_program(g, core, T, topo):
@@ -87,9 +100,9 @@ def rank_program(g, core, T, topo):
         forward(g, core, T, topo)
         return
     sem = T.sem
-    far0 = T.cores[rank ^ ORDER[0]]
-    off = topo.engines(core, far0)
+    off = off_chip(rank, T, topo)
     half = len(off) // 2
+    rest = [e for e in topo.engines(core, T.cores[rank ^ ORDER[6]]) if e not in off]
     COPY = ActivationFunctionType.Copy
 
     g.sync.dma_start(T.cwi[:], T.cw[:]).then_inc(sem.ldc, 16)
@@ -98,14 +111,9 @@ def rank_program(g, core, T, topo):
 
     g.wait_ge(sem.conv, 1)
     lsent = 0
-    mate = T.cores[rank ^ ORDER[6]]
-    rest = relay_engines(core, mate, far0, topo)
-    for i in range(3):
-        part = [(STEPS[i][0], off[:half]), (STEPS[i][1], off[half:])]
-        if i == 2:
-            part.append((6, rest))
+    for call in LISTS:
         tr = []
-        for slot, eng in part:
+        for slot, eng in zip(call, (off[:half], off[half:], rest)):
             p = rank ^ ORDER[slot]
             tr.append(RemoteDMATransfer(dst_ids=[dest(T.cores[p], topo)], dma_engine_mask=bits(eng),
                                         remote_sem=sem["l%d" % slot], src=T.cwu[:, p * L:p * L + L],
@@ -115,13 +123,15 @@ def rank_program(g, core, T, topo):
     g.sync.wait_ge(sem.lsent, lsent)
     g.sync.dma_start(T.xs[:, h:2 * h], T.x[:, h:2 * h]).then_inc(sem.ldx1, 16)
 
+    def listed(queue, slot):
+        queue.wait_ge(sem["l%d" % slot], half if slot < 6 else len(rest))
+
     wsent = 0
     for i, step in enumerate(STEPS):
         g.wait_ge(sem["q%d" % i], 1)
         for what in range(2):
             tr = []
             for slot in step:
-                dst = T.cores[rank ^ ORDER[slot]]
                 via = relay_of(rank, slot, T, topo)
                 a = (slot + 1) * S
                 if what == 0:
@@ -129,11 +139,10 @@ def rank_program(g, core, T, topo):
                 else:
                     src, out = T.wz[:, a:a + S], T.rz[:, slot * S:slot * S + S]
                 if via is None:
-                    to, s = dst, sem["a%d" % slot]
-                    eng = rest if slot == 6 else off
+                    to, s = T.cores[rank ^ ORDER[slot]], sem["a%d" % slot]
                 else:
                     to, s = via, sem[("rc%d" if what == 0 else "rz%d") % slot]
-                    eng = relay_engines(core, via, dst, topo)
+                eng = first_engines(rank, slot, T, topo)
                 tr.append(RemoteDMATransfer(dst_ids=[dest(to, topo)], dma_engine_mask=bits(eng), remote_sem=s,
                                             src=src, dst=out))
                 wsent += len(eng)
@@ -152,6 +161,14 @@ def rank_program(g, core, T, topo):
         a = (slot + 1) * 4 * S
         return T.w[:, a + t:a + n * 4 * S:4]
 
+    def gathers(i, scalar):
+        step, mine = STEPS[i], SHARE[i]
+        if len(step) == 1:
+            return [(t, step[0], 1) for t in range(4) if (t in mine) == scalar]
+        if scalar:
+            return [(2, step[0], 2), (3, step[0], 2), (1, step[1], 1)]
+        return [(0, step[0], 2), (1, step[0], 1)]
+
     mylist = T.cwu[:, rank * L:rank * L + L]
     g.scalar.wait_ge(sem.pls, 2)
     g.scalar.wait_ge(sem.conv, 1)
@@ -159,15 +176,10 @@ def rank_program(g, core, T, topo):
         g.scalar.activation(place(t, -1, 1), window(t).indirect(mylist), COPY).then_inc(sem.gss, 1)
     g.scalar.wait_ge(sem.plv, 2)
     for i, step in enumerate(STEPS):
-        n, a = len(step), step[0]
         for slot in step:
-            g.scalar.wait_ge(sem["l%d" % slot], half if slot < 6 else len(rest))
-        lists = T.lst[:, a * L:(a + n) * L]
-        for t in (2, 3):
-            g.scalar.activation(place(t, a, n), window(t).indirect(lists), COPY).then_inc(sem["gs%d" % i], 1)
-        if n == 2:
-            b = step[1]
-            g.scalar.activation(place(1, b, 1), window(1).indirect(T.lst[:, b * L:b * L + L]), COPY).then_inc(sem["gs%d" % i], 1)
+            listed(g.scalar, slot)
+        for t, a, n in gathers(i, True):
+            g.scalar.activation(place(t, a, n), window(t).indirect(T.lst[:, a * L:(a + n) * L]), COPY).then_inc(sem["gs%d" % i], 1)
 
     g.vector.wait_ge(sem.ldc, 16)
     g.vector.tensor_copy(T.cwu[:], T.cwi[:]).then_inc(sem.conv, 1)
@@ -189,15 +201,15 @@ def rank_program(g, core, T, topo):
 
     quantise_x(0)
     for i, step in enumerate(STEPS):
-        n, a = len(step), step[0]
-        if i == 3:
+        if i == len(STEPS) - 1:
             quantise_x(1)
         for slot in step:
-            g.vector.wait_ge(sem["l%d" % slot], half if slot < 6 else len(rest))
-        g.vector.tensor_copy(place(0, a, n), window(0).indirect(T.lst[:, a * L:(a + n) * L])).then_inc(sem["gv%d" % i], 1)
-        g.vector.tensor_copy(place(1, a, 1), window(1).indirect(T.lst[:, a * L:a * L + L])).then_inc(sem["gv%d" % i], 1)
-        g.vector.wait_ge(sem["gv%d" % i], 2)
-        g.vector.wait_ge(sem["gs%d" % i], 2 if n == 1 else 3)
+            listed(g.vector, slot)
+        for t, a, n in gathers(i, False):
+            g.vector.tensor_copy(place(t, a, n), window(t).indirect(T.lst[:, a * L:(a + n) * L])).then_inc(sem["gv%d" % i], 1)
+        g.vector.wait_ge(sem["gv%d" % i], len(gathers(i, False)))
+        g.vector.wait_ge(sem["gs%d" % i], len(gathers(i, True)))
+        a, n = step[0], len(step)
         c = slice((a + 1) * S, (a + 1 + n) * S)
         g.vector.quantize_mx(T.wq[:, c], T.wz[:, c],
                              T.w[:, (a + 1) * 4 * S:(a + 1 + n) * 4 * S]).then_inc(sem["q%d" % i], 1)
@@ -213,12 +225,12 @@ def rank_program(g, core, T, topo):
     g.tensor.wait_ge(sem.qself, 1)
     product(rank, T.wq[:, 0:S], T.wz[:, 0:S], True, False)
     for j, slot in enumerate(ARRIVAL):
-        via = relay_of(rank ^ ORDER[slot], slot, T, topo)
-        src = T.cores[rank ^ ORDER[slot]]
-        count = len(rest) if slot == 6 else len(topo.engines(src if via is None else via, core))
+        p = rank ^ ORDER[slot]
+        via = relay_of(p, slot, T, topo)
+        count = len(first_engines(p, slot, T, topo) if via is None else topo.engines(via, core))
         g.tensor.wait_ge(sem["a%d" % slot], 2 * count)
         c = slice(slot * S, slot * S + S)
-        product(rank ^ ORDER[slot], T.rq[:, c], T.rz[:, c], False, j == 6)
+        product(p, T.rq[:, c], T.rz[:, c], False, j == 6)
 
     g.vector.wait_ge(sem.mm, 1)
     g.vector.tensor_copy(T.ys[:], T.yp[:, 0:S]).then_inc(sem.cp, 1)

from concourse.mybir import dt, AluOpType, ActivationFunctionType
from concourse.bass import DstId, RemoteDMATransfer

N = 8
S = 256
L = S // 16
ORDER = (3, 2, 5, 7, 6, 4, 1)
VIA = (True, False, True, True, False, False, False)
STEPS = ((0,), (1, 2), (3,), (4,), (5,), (6,))
SHARE = ((2, 3), (2, 3, 1), (1, 2, 3), (2, 3), (1, 2, 3), (2, 3))
LISTS = ((0, 1), (2, 3), (4, 5, 6))
ARRIVAL = (1, 0, 2, 4, 3, 6, 5)

SCRATCH = {
    "cwi": ("sbuf", [128, N * L], "int32"),
    "cwu": ("sbuf", [128, N * L], "uint16"),
    "lst": ("sbuf", [128, 7 * L], "uint16"),
    "bks": ("sbuf", [128, 512], "bfloat16"),
    "bkp": ("sbuf", [128, 512], "bfloat16"),
    "xs": ("sbuf", [128, 512 * N], "bfloat16"),
    "xq": ("sbuf", [128, 128 * N], "float8_e4m3fn_x4"),
    "xz": ("sbuf", [128, 128 * N], "uint8"),
    "w": ("sbuf", [128, 4 * S * N], "bfloat16"),
    "wq": ("sbuf", [128, S * N], "float8_e4m3fn_x4"),
    "wz": ("sbuf", [128, S * N], "uint8"),
    "rq": ("sbuf", [128, S * 7], "float8_e4m3fn_x4"),
    "rz": ("sbuf", [128, S * 7], "uint8"),
    "yp": ("psum", [128, 512], "float32"),
    "ys": ("sbuf", [128, S], "float32"),
}
SEMAPHORES = (["ldc", "ldb", "ldx0", "ldx1", "conv", "plv", "pls", "lsent", "wsent", "fsent", "qself", "gvs", "gss",
               "xq0", "xq1", "mm", "cp", "st"]
              + ["l%d" % k for k in range(7)] + ["a%d" % k for k in range(7)]
              + ["rc%d" % k for k in range(7)] + ["rz%d" % k for k in range(7)]
              + ["gv%d" % i for i in range(6)] + ["gs%d" % i for i in range(6)] + ["q%d" % i for i in range(6)])


def bits(engines):
    return sum(1 << e for e in engines)


def dest(core, topo):
    rid, pid, _ = topo.addr(core)
    return DstId(rid=rid, pnc=pid)


def relay_of(rank, slot, T, topo):
    if not VIA[slot]:
        return None
    src, dst = T.cores[rank], T.cores[rank ^ ORDER[slot]]
    cand = [c for c in topo.cores_of(src)
            if T.rank_of(c) is None and topo.may_write(c, dst) and topo.die(c) != topo.die(src)]
    reach = {c: sum(topo.may_write(c, d) for d in T.cores) for c in cand}
    cand = [c for c in cand if reach[c] == min(reach.values())]
    mine = [c for c in T.cores if topo.chip(c) == topo.chip(src)]
    return cand[mine.index(src) % len(cand)]


def off_chip(rank, T, topo):
    return topo.engines(T.cores[rank], T.cores[rank ^ ORDER[0]])


def first_engines(rank, slot, T, topo):
    src, dst = T.cores[rank], T.cores[rank ^ ORDER[slot]]
    off = off_chip(rank, T, topo)
    via = relay_of(rank, slot, T, topo)
    to = dst if via is None else via
    if topo.chip(src) != topo.chip(to):
        return off
    engines = topo.engines(src, to)
    return engines if slot == 0 else [e for e in engines if e not in off]


def forward(g, core, T, topo):
    total = 0
    for slot in range(7):
        for rank in range(N):
            if relay_of(rank, slot, T, topo) != core:
                continue
            dst = T.cores[rank ^ ORDER[slot]]
            rid, pid, _ = topo.addr(dst)
            mask = topo.mask(core, dst)
            came = len(first_engines(rank, slot, T, topo))
            c = slice(slot * S, slot * S + S)
            view = T.rq[:, c].bitcast(dt.uint8)
            g.wait_ge(T.sem["rc%d" % slot], came)
            g.remote_dma(out_ap=view, in_ap=view, remote_sem=T.sem["a%d" % slot], local_sem=T.sem.fsent,
                         pid=pid, routing_id=rid, dma_engine_mask=mask)
            g.wait_ge(T.sem["rz%d" % slot], came)
            g.remote_dma(out_ap=T.rz[:, c], in_ap=T.rz[:, c], remote_sem=T.sem["a%d" % slot], local_sem=T.sem.fsent,
                         pid=pid, routing_id=rid, dma_engine_mask=mask)
            total += 2 * len(topo.engines(core, dst))
    if total:
        g.wait_ge(T.sem.fsent, total)


def rank_program(g, core, T, topo):
    rank = T.rank_of(core)
    if rank is None:
        forward(g, core, T, topo)
        return
    sem = T.sem
    off = off_chip(rank, T, topo)
    half = len(off) // 2
    rest = [e for e in topo.engines(core, T.cores[rank ^ ORDER[6]]) if e not in off]
    COPY = ActivationFunctionType.Copy

    g.sync.dma_start(T.cwi[:], T.cw[:]).then_inc(sem.ldc, 16)
    h = 512 * N // 2
    g.sync.dma_start(T.xs[:, 0:h], T.x[:, 0:h]).then_inc(sem.ldx0, 16)

    g.wait_ge(sem.conv, 1)
    lsent = 0
    for call in LISTS:
        tr = []
        for slot, eng in zip(call, (off[:half], off[half:], rest)):
            p = rank ^ ORDER[slot]
            tr.append(RemoteDMATransfer(dst_ids=[dest(T.cores[p], topo)], dma_engine_mask=bits(eng),
                                        remote_sem=sem["l%d" % slot], src=T.cwu[:, p * L:p * L + L],
                                        dst=T.lst[:, slot * L:slot * L + L]))
            lsent += len(eng)
        g.remote_dma_fused(tr, local_sem=sem.lsent)
    g.sync.wait_ge(sem.lsent, lsent)
    g.sync.dma_start(T.xs[:, h:2 * h], T.x[:, h:2 * h]).then_inc(sem.ldx1, 16)

    def listed(queue, slot):
        queue.wait_ge(sem["l%d" % slot], half if slot < 6 else len(rest))

    wsent = 0
    for i, step in enumerate(STEPS):
        g.wait_ge(sem["q%d" % i], 1)
        for what in range(2):
            tr = []
            for slot in step:
                via = relay_of(rank, slot, T, topo)
                a = (slot + 1) * S
                if what == 0:
                    src, out = T.wq[:, a:a + S].bitcast(dt.uint8), T.rq[:, slot * S:slot * S + S].bitcast(dt.uint8)
                else:
                    src, out = T.wz[:, a:a + S], T.rz[:, slot * S:slot * S + S]
                if via is None:
                    to, s = T.cores[rank ^ ORDER[slot]], sem["a%d" % slot]
                else:
                    to, s = via, sem[("rc%d" if what == 0 else "rz%d") % slot]
                eng = first_engines(rank, slot, T, topo)
                tr.append(RemoteDMATransfer(dst_ids=[dest(to, topo)], dma_engine_mask=bits(eng), remote_sem=s,
                                            src=src, dst=out))
                wsent += len(eng)
            g.remote_dma_fused(tr, local_sem=sem.wsent)
    g.wait_ge(sem.wsent, wsent)

    g.scalar.dma_start(T.bks[:], T.bk[:]).then_inc(sem.ldb, 16)
    g.scalar.wait_ge(sem.ldb, 16)
    for t in (2, 3):
        g.scalar.activation(T.bkp[:, t * 128:t * 128 + 128], T.bks[:, t:512:4], COPY).then_inc(sem.pls, 1)

    def window(t):
        return T.bkp[:, t * 128:t * 128 + 128]

    def place(t, slot, n):
        a = (slot + 1) * 4 * S
        return T.w[:, a + t:a + n * 4 * S:4]

    def gathers(i, scalar):
        step, mine = STEPS[i], SHARE[i]
        if len(step) == 1:
            return [(t, step[0], 1) for t in range(4) if (t in mine) == scalar]
        if scalar:
            return [(2, step[0], 2), (3, step[0], 2), (1, step[1], 1)]
        return [(0, step[0], 2), (1, step[0], 1)]

    mylist = T.cwu[:, rank * L:rank * L + L]
    g.scalar.wait_ge(sem.pls, 2)
    g.scalar.wait_ge(sem.conv, 1)
    for t in (2, 3):
        g.scalar.activation(place(t, -1, 1), window(t).indirect(mylist), COPY).then_inc(sem.gss, 1)
    g.scalar.wait_ge(sem.plv, 2)
    for i, step in enumerate(STEPS):
        for slot in step:
            listed(g.scalar, slot)
        for t, a, n in gathers(i, True):
            g.scalar.activation(place(t, a, n), window(t).indirect(T.lst[:, a * L:(a + n) * L]), COPY).then_inc(sem["gs%d" % i], 1)

    g.vector.wait_ge(sem.ldc, 16)
    g.vector.tensor_copy(T.cwu[:], T.cwi[:]).then_inc(sem.conv, 1)
    g.vector.wait_ge(sem.ldb, 16)
    for t in (0, 1):
        g.vector.tensor_copy(T.bkp[:, t * 128:t * 128 + 128], T.bks[:, t:512:4]).then_inc(sem.plv, 1)
    g.vector.wait_ge(sem.plv, 2)
    g.vector.wait_ge(sem.conv, 1)
    for t in (0, 1):
        g.vector.tensor_copy(place(t, -1, 1), window(t).indirect(mylist)).then_inc(sem.gvs, 1)
    g.vector.wait_ge(sem.gvs, 2)
    g.vector.wait_ge(sem.gss, 2)
    g.vector.quantize_mx(T.wq[:, 0:S], T.wz[:, 0:S], T.w[:, 0:4 * S]).then_inc(sem.qself, 1)

    def quantise_x(b):
        g.vector.wait_ge(sem["ldx%d" % b], 16)
        c = slice(b * 512, b * 512 + 512)
        g.vector.quantize_mx(T.xq[:, c], T.xz[:, c], T.xs[:, b * 2048:b * 2048 + 2048]).then_inc(sem["xq%d" % b], 1)

    quantise_x(0)
    for i, step in enumerate(STEPS):
        if i == len(STEPS) - 1:
            quantise_x(1)
        for slot in step:
            listed(g.vector, slot)
        for t, a, n in gathers(i, False):
            g.vector.tensor_copy(place(t, a, n), window(t).indirect(T.lst[:, a * L:(a + n) * L])).then_inc(sem["gv%d" % i], 1)
        g.vector.wait_ge(sem["gv%d" % i], len(gathers(i, False)))
        g.vector.wait_ge(sem["gs%d" % i], len(gathers(i, True)))
        a, n = step[0], len(step)
        c = slice((a + 1) * S, (a + 1 + n) * S)
        g.vector.quantize_mx(T.wq[:, c], T.wz[:, c],
                             T.w[:, (a + 1) * 4 * S:(a + 1 + n) * 4 * S]).then_inc(sem["q%d" % i], 1)

    def product(s, codes, scales, start, stop):
        c = slice(s * 128, s * 128 + 128)
        r = g.tensor.matmul_mx(T.yp[:, 0:S], T.xq[:, c], T.xz[:, c], codes, scales, start, stop)
        if stop:
            r.then_inc(sem.mm, 1)

    g.tensor.wait_ge(sem.xq0, 1)
    g.tensor.wait_ge(sem.xq1, 1)
    g.tensor.wait_ge(sem.qself, 1)
    product(rank, T.wq[:, 0:S], T.wz[:, 0:S], True, False)
    for j, slot in enumerate(ARRIVAL):
        p = rank ^ ORDER[slot]
        via = relay_of(p, slot, T, topo)
        count = len(first_engines(p, slot, T, topo) if via is None else topo.engines(via, core))
        g.tensor.wait_ge(sem["a%d" % slot], 2 * count)
        c = slice(slot * S, slot * S + S)
        product(p, T.rq[:, c], T.rz[:, c], False, j == 6)

    g.vector.wait_ge(sem.mm, 1)
    g.vector.tensor_copy(T.ys[:], T.yp[:, 0:S]).then_inc(sem.cp, 1)
    g.sync.wait_ge(sem.cp, 1)
    g.sync.dma_start(T.y[:], T.ys[:]).then_inc(sem.st, 16)
    g.sync.wait_ge(sem.st, 16)
